import numpy as np
import ml_dtypes


def mxq(x, axis, fmt="e4m3"):
    dtype, down = {"e4m3": (ml_dtypes.float8_e4m3fn, 7), "e5m2": (ml_dtypes.float8_e5m2, 14)}[fmt]
    v = np.moveaxis(np.asarray(x, np.float32).astype(ml_dtypes.bfloat16).astype(np.float64), axis, -1)
    blocks = v.reshape(v.shape[:-1] + (-1, 32))
    amax = np.abs(blocks).max(-1, keepdims=True)
    byte = np.maximum(np.where(amax > 0, np.frexp(amax)[1] - 1 + 127, 0) - down, 1)
    scale = np.exp2(byte - 127.0)
    codes = (blocks / scale).astype(np.float32).astype(dtype).astype(np.float64)
    return np.moveaxis((codes * scale).reshape(v.shape), -1, axis)


WIDE = False


def mx_kscale(k):
    if not WIDE:
        return np.ones(k)
    levels = np.array([10, -10, 5, -5, 0])
    if k % 512:
        return np.exp2(np.random.permutation(np.resize(levels, k // 32))).repeat(32)
    a = np.empty((k // 512, 16))
    for p in range(k // 512):
        a[p, :8] = np.random.permutation(np.resize(levels, 8))
        for g in range(8):
            far = levels[np.abs(levels - a[p, g]) >= 10]
            a[p, g + 8] = far[np.random.randint(len(far))]
    return np.exp2(a.ravel()).repeat(32)


def f64(x):
    return np.asarray(x).astype(np.float64)


def striped(idx):
    return np.tile(idx.reshape(-1, 16).T, (8, 1)).astype(np.uint16)


def unstriped(offs):
    return offs[:16].T.reshape(-1).astype(np.int64)


def pack_weight(w):
    k, n = w.shape
    w = f64(np.asarray(w, np.float32).astype(ml_dtypes.bfloat16)).reshape(k // 32, 32, n)
    amax = np.abs(w).max(1)
    byte = np.clip(np.where(amax > 0, np.frexp(amax)[1] - 1 + 127 - 7, 1), 1, 254)
    scaled = (w * np.exp2(127.0 - byte)[:, None, :]).reshape(k, n).astype(np.float32)
    words = np.ascontiguousarray(scaled.reshape(k // 512, 128, 4, n).transpose(0, 1, 3, 2)).astype(ml_dtypes.float8_e4m3fn).view(np.uint8)
    return words, np.ascontiguousarray(byte.astype(np.uint8).reshape(k // 512, 16, n))


def unpack_weight(words, scales):
    g, p, n, _ = words.shape
    vals = np.ascontiguousarray(words).view(ml_dtypes.float8_e4m3fn).astype(np.float64) * np.repeat(np.exp2(scales.astype(np.float64) - 127.0), 8, axis=1)[..., None]
    return vals.transpose(0, 1, 3, 2).reshape(g * 512, n)


K, T, S, D, N, H, V, U = 512, 2048, 1024, 4, 128, 512, 256, 512


def setup_inputs():
    n = np.random.standard_normal
    s = mx_kscale(K)[:, None]
    u = mx_kscale(H)
    packed_xT = pack_weight(n((K, T)) * s)
    return {
        "x_words": packed_xT[0],
        "x_scales": packed_xT[1],
        "w1": (n((K, H)) / np.sqrt(K) / s).astype(np.float32),
        "shp": (np.random.uniform(0.0, 1.0, (H, U))).astype(np.float32),
        "unit": (np.random.uniform(0.6, 1.4, (H, 1)) * u[:, None]).astype(np.float32),
        "w2": (n((H, N)) / np.sqrt(H) / u[:, None]).astype(np.float32),
        "offs": striped(np.random.permutation(T)[:S]),
        "fa": striped(np.random.permutation(np.concatenate([np.arange(V), np.random.randint(0, V, U - V)]))),
        "fb": striped(np.random.permutation(np.concatenate([np.arange(V), np.random.randint(0, V, U - V)]))),
        "va": striped(np.random.randint(0, S, U)),
        "vb": striped(np.random.randint(0, S, U)),
    }


def reference(x_words, x_scales, w1, shp, unit, w2, offs, fa, fb, va, vb):
    xq = unpack_weight(x_words, x_scales)[:, unstriped(offs)]
    y = mxq(f64(w1), 0, "e4m3").T @ xq
    pa = y[:, unstriped(va)]
    pb = y[:, unstriped(vb)]
    mid = pa + pb
    face = y.reshape(len(y), -1, D).mean(axis=2)
    edge = 0.25 * (mid + face[:, unstriped(fa)] + face[:, unstriped(fb)])
    ept = f64(shp) * (0.5 * mid) + (-1.0 * f64(shp) + 1.0) * edge
    hid = f64(unit) * ept
    return mxq(f64(w2), 0, "e4m3").T @ mxq(hid, 0, "e4m3")

@@ -1,0 +1,238 @@
+from contextlib import ExitStack
+
+import concourse.mybir as mybir
+
+K, T, S, D, N, H, V, U = 512, 2048, 1024, 4, 128, 512, 256, 512
+FLOPS = 2 * K * H * S + 2 * H * N * U
+
+F32 = mybir.dt.float32
+BF16 = mybir.dt.bfloat16
+I32 = mybir.dt.int32
+U32 = mybir.dt.uint32
+U16 = mybir.dt.uint16
+U8 = mybir.dt.uint8
+FP8X4 = mybir.dt.float8_e4m3fn_x4
+ADD, SUB, MULT = mybir.AluOpType.add, mybir.AluOpType.subtract, mybir.AluOpType.mult
+COPY = mybir.ActivationFunctionType.Copy
+
+P = 128
+PACK = 4
+BANK = 512
+HALF = U // 2
+W1_CHUNK = H // 2
+
+
+def tile_picked_ycatmu_pos_p_kernel(
+    tc, x_words, x_scales, w1, shp, unit, w2, offs, fa, fb, va, vb, out
+):
+    nc = tc.nc
+    with ExitStack() as ctx:
+        keep = ctx.enter_context(tc.tile_pool(name="keep", bufs=1))
+        psum = ctx.enter_context(tc.psum_pool(name="psum", bufs=1))
+
+        def tile(shape, dtype, name):
+            return keep.tile(shape, dtype, name=name, align_bytes=64)
+
+        def load_list(src, name):
+            dst = tile([P, src.shape[1]], U16, name)
+            nc.sync.dma_start(out=dst[:], in_=src)
+            return dst
+
+        table_scales = tile([P, T], U8, "table_scales")
+        nc.vector.memset(table_scales[:].bitcast(I32), 0)
+        offs_sb = load_list(offs, "offs_sb")
+        w1_rows = w1.rearrange("(p j) c -> p j c", j=PACK)
+        w1_raw = [tile([P, PACK, W1_CHUNK], F32, f"w1_raw{c}") for c in range(2)]
+        nc.sync.dma_start(out=w1_raw[0][:], in_=w1_rows[:, :, 0:W1_CHUNK])
+        for q in range(4):
+            nc.scalar.dma_start(
+                out=table_scales[32 * q : 32 * q + 4, :].bitcast(I32),
+                in_=x_scales[0, 4 * q : 4 * q + 4, :].bitcast(I32),
+            )
+        table_words = tile([P, T], I32, "table_words")
+        nc.sync.dma_start(out=table_words[:], in_=x_words[0].rearrange("p c r -> p (c r)").bitcast(I32))
+        nc.sync.dma_start(out=w1_raw[1][:], in_=w1_rows[:, :, W1_CHUNK:H])
+        unit_sb = tile([P, PACK], F32, "unit_sb")
+        nc.sync.dma_start(out=unit_sb[:], in_=unit.rearrange("(p t) o -> p (t o)", t=PACK))
+        w2_raw = tile([P, PACK, N], F32, "w2_raw")
+        nc.sync.dma_start(out=w2_raw[:], in_=w2.rearrange("(p j) n -> p j n", j=PACK))
+        va_sb = load_list(va, "va_sb")
+        vb_sb = load_list(vb, "vb_sb")
+        fa_sb = load_list(fa, "fa_sb")
+        fb_sb = load_list(fb, "fb_sb")
+        shp_rows = shp.rearrange("(p t) r -> p t r", t=PACK)
+        shp_sb = [tile([P, 2, U], F32, f"shp_sb{u}") for u in range(2)]
+        for u in range(2):
+            nc.sync.dma_start(out=shp_sb[u][:], in_=shp_rows[:, 2 * u : 2 * u + 2, :])
+
+        x_scale = tile([P, S], U8, "x_scale")
+        nc.vector.tensor_copy(x_scale[:], table_scales[:].indirect(offs_sb[:]))
+        x_code = [tile([P, BANK], U32, f"x_code{b}") for b in range(2)]
+        for b in range(2):
+            nc.vector.tensor_copy(
+                x_code[b][:], table_words[:].bitcast(U32).indirect(offs_sb[:, 32 * b : 32 * b + 32])
+            )
+
+        w1_bf = tile([P, PACK, P, PACK], BF16, "w1_bf")
+        for c in range(2):
+            nc.scalar.activation(
+                out=w1_bf[:, :, 64 * c : 64 * c + 64, :].rearrange("p t m j -> p m j t"),
+                in_=w1_raw[c][:].rearrange("p j (m t) -> p m j t", t=PACK),
+                func=COPY,
+            )
+        w1_code = tile([P, H], U32, "w1_code")
+        w1_scale = tile([P, H], U8, "w1_scale")
+        for t in range(PACK):
+            nc.vector.quantize_mx(
+                out=w1_code[:, P * t : P * (t + 1)].bitcast(FP8X4),
+                scales=w1_scale[:, P * t : P * (t + 1)],
+                in_=w1_bf[:, t, :, :].rearrange("p m j -> p (m j)"),
+            )
+        gain = tile([P, PACK], F32, "gain")
+        nc.gpsimd.tensor_scalar(gain[:], unit_sb[:], 0.0625, 0.0, MULT, ADD)
+
+        y_psum = {}
+        for t in range(PACK):
+            for b in range(2):
+                y_psum[t, b] = psum.tile([P, BANK], F32, name=f"bank{2 * t + b}")
+                nc.tensor.matmul_mx(
+                    out=y_psum[t, b][:],
+                    lhsT=w1_code[:, P * t : P * (t + 1)].bitcast(FP8X4),
+                    lhsT_scale=w1_scale[:, P * t : P * (t + 1)],
+                    rhs=x_code[b][:].bitcast(FP8X4),
+                    rhs_scale=x_scale[:, BANK * b : BANK * (b + 1)],
+                    start=True,
+                    stop=True,
+                )
+
+        w2_bf = tile([P, N, PACK], BF16, "w2_bf")
+        nc.vector.tensor_copy(w2_bf[:], w2_raw[:].rearrange("p j n -> p n j"))
+        w2_code = tile([P, N], U32, "w2_code")
+        w2_scale = tile([P, N], U8, "w2_scale")
+
+        y = [tile([P, S], F32, f"y{t}") for t in range(PACK)]
+        face = [tile([P, V + 2 * V], F32, f"face{t}") for t in range(PACK)]
+
+        def evacuate(t, b, on_vector):
+            dst = y[t][:, BANK * b : BANK * (b + 1)]
+            if on_vector:
+                nc.vector.tensor_scalar(dst, y_psum[t, b][:], gain[:, t : t + 1], None, MULT)
+            else:
+                nc.scalar.activation(out=dst, in_=y_psum[t, b][:], func=COPY, scale=gain[:, t : t + 1])
+
+        def face_pairs(t):
+            quads = y[t][:].rearrange("p (v d) -> p v d", d=D)
+            nc.vector.tensor_tensor(
+                face[t][:, V : 3 * V].rearrange("p (v e) -> p v e", e=2), quads[:, :, 0:2], quads[:, :, 2:4], ADD
+            )
+
+        def face_sums(t):
+            nc.vector.tensor_tensor(face[t][:, 0:V], face[t][:, V : 3 * V : 2], face[t][:, V + 1 : 3 * V : 2], ADD)
+
+        def unit_tiles(name, dtype):
+            return {(u, h): tile([P, 2, HALF], dtype, f"{name}{u}{h}") for u in range(2) for h in range(2)}
+
+        pa, pb, ga, gb = unit_tiles("pa", F32), unit_tiles("pb", F32), unit_tiles("ga", F32), unit_tiles("gb", F32)
+        mid, part, diff, mix = unit_tiles("mid", F32), unit_tiles("part", F32), unit_tiles("diff", F32), unit_tiles("mix", F32)
+        hid_pairs = [tile([P, 2, HALF, 2], BF16, f"hid_pairs{h}") for h in range(2)]
+
+        def cols(lst, h):
+            return lst[:, 16 * h : 16 * h + 16]
+
+        def gather(dst, window, lst, t, h):
+            nc.scalar.activation(out=dst[t // 2, h][:, t % 2, :], in_=window[t][:].indirect(cols(lst, h)), func=COPY)
+
+        def add_mid(u, h, ts):
+            nc.vector.tensor_tensor(mid[u, h][:, ts, :], pa[u, h][:, ts, :], pb[u, h][:, ts, :], ADD)
+
+        def sub_mid(u, h, ts):
+            nc.vector.scalar_tensor_tensor(part[u, h][:, ts, :], mid[u, h][:, ts, :], -4.0, ga[u, h][:, ts, :], MULT, ADD)
+
+        def add_face_fused(t, h):
+            u = t // 2
+            nc.vector.tensor_tensor(diff[u, h][:, t % 2, :], face[t][:].indirect(cols(fb_sb, h)), part[u, h][:, t % 2, :], ADD)
+
+        def add_face(u, h):
+            nc.vector.tensor_tensor(diff[u, h][:], gb[u, h][:], part[u, h][:], ADD)
+
+        def sharpen(u, h):
+            nc.vector.scalar_tensor_tensor(
+                mix[u, h][:], shp_sb[u][:, :, HALF * h : HALF * (h + 1)], -1.0, diff[u, h][:], ADD, MULT
+            )
+
+        def round_pairs(u, h):
+            nc.vector.scalar_tensor_tensor(
+                hid_pairs[h][:, u, :, :],
+                mid[u, h][:].rearrange("p e r -> p r e"),
+                8.0,
+                mix[u, h][:].rearrange("p e r -> p r e"),
+                MULT,
+                SUB,
+            )
+
+        def decode(h):
+            hid_bf = tile([P, HALF, PACK], BF16, f"hid_bf{h}")
+            nc.vector.tensor_copy(
+                hid_bf[:].rearrange("p r t -> p (r t)").bitcast(I32).rearrange("p (r u) -> p r u", u=2),
+                hid_pairs[h][:].rearrange("p u r e -> p (u r e)").bitcast(I32).rearrange("p (u r) -> p r u", u=2),
+            )
+            hid_code = tile([P, HALF], U32, f"hid_code{h}")
+            hid_scale = tile([P, HALF], U8, f"hid_scale{h}")
+            nc.vector.quantize_mx(
+                out=hid_code[:].bitcast(FP8X4), scales=hid_scale[:], in_=hid_bf[:].rearrange("p r t -> p (r t)")
+            )
+            acc = psum.tile([P, BANK], F32, name=f"bank{h}")
+            nc.tensor.matmul_mx(
+                out=acc[:, 0:HALF],
+                lhsT=w2_code[:].bitcast(FP8X4),
+                lhsT_scale=w2_scale[:],
+                rhs=hid_code[:].bitcast(FP8X4),
+                rhs_scale=hid_scale[:],
+                start=True,
+                stop=True,
+            )
+            res = tile([P, HALF], F32, f"res{h}")
+            nc.scalar.activation(out=res[:], in_=acc[:, 0:HALF], func=COPY)
+            nc.sync.dma_start(out=out[:, HALF * h : HALF * (h + 1)], in_=res[:])
+
+        evacuate(0, 0, False)
+        evacuate(0, 1, True)
+        nc.vector.quantize_mx(
+            out=w2_code[:].bitcast(FP8X4), scales=w2_scale[:], in_=w2_bf[:].rearrange("p n j -> p (n j)")
+        )
+        for t in range(PACK):
+            u, one = t // 2, slice(t % 2, t % 2 + 1)
+            face_pairs(t)
+            gather(pa, y, va_sb, t, 0)
+            gather(pb, y, vb_sb, t, 0)
+            if t == 0:
+                evacuate(1, 0, True)
+            face_sums(t)
+            if t == 0:
+                evacuate(1, 1, True)
+            gather(ga, face, fa_sb, t, 0)
+            if 0 < t < PACK - 1:
+                evacuate(t + 1, 0, False)
+                evacuate(t + 1, 1, False)
+            add_mid(u, 0, one)
+            sub_mid(u, 0, one)
+            add_face_fused(t, 0)
+            if t % 2 == 1:
+                sharpen(u, 0)
+                round_pairs(u, 0)
+        decode(0)
+        both = slice(0, 2)
+        for u in range(2):
+            for t in (2 * u, 2 * u + 1):
+                gather(pa, y, va_sb, t, 1)
+                gather(pb, y, vb_sb, t, 1)
+            add_mid(u, 1, both)
+            for t in (2 * u, 2 * u + 1):
+                gather(ga, face, fa_sb, t, 1)
+            sub_mid(u, 1, both)
+            for t in (2 * u, 2 * u + 1):
+                gather(gb, face, fb_sb, t, 1)
+            add_face(u, 1)
+            sharpen(u, 1)
+            round_pairs(u, 1)
+        decode(1)

@@ -18,7 +18,7 @@ COPY = mybir.ActivationFunctionType.Copy
 P = 128
 PACK = 4
 BANK = 512
-HALF = U // 2
+PIECES = ((0, 256), (256, 256))
 W1_CHUNK = H // 2
 
 
@@ -28,6 +28,7 @@ def tile_picked_ycatmu_pos_p_kernel(
     nc = tc.nc
     with ExitStack() as ctx:
         keep = ctx.enter_context(tc.tile_pool(name="keep", bufs=1))
+        ring = ctx.enter_context(tc.tile_pool(name="ring", bufs=2))
         psum = ctx.enter_context(tc.psum_pool(name="psum", bufs=1))
 
         def tile(shape, dtype, name):
@@ -38,20 +39,19 @@ def tile_picked_ycatmu_pos_p_kernel(
             nc.sync.dma_start(out=dst[:], in_=src)
             return dst
 
-        table_scales = tile([P, T], U8, "table_scales")
-        nc.vector.memset(table_scales[:].bitcast(I32), 0)
         offs_sb = load_list(offs, "offs_sb")
-        w1_rows = w1.rearrange("(p j) c -> p j c", j=PACK)
-        w1_raw = [tile([P, PACK, W1_CHUNK], F32, f"w1_raw{c}") for c in range(2)]
-        nc.sync.dma_start(out=w1_raw[0][:], in_=w1_rows[:, :, 0:W1_CHUNK])
+        table_scales = tile([P, T], U8, "table_scales")
         for q in range(4):
-            nc.scalar.dma_start(
-                out=table_scales[32 * q : 32 * q + 4, :].bitcast(I32),
-                in_=x_scales[0, 4 * q : 4 * q + 4, :].bitcast(I32),
+            nc.sync.dma_start(
+                out=table_scales[32 * q : 32 * q + 32, :].bitcast(I32),
+                in_=x_scales[0, 4 * q : 4 * q + 4, :].bitcast(I32).partition_broadcast(8),
             )
         table_words = tile([P, T], I32, "table_words")
         nc.sync.dma_start(out=table_words[:], in_=x_words[0].rearrange("p c r -> p (c r)").bitcast(I32))
-        nc.sync.dma_start(out=w1_raw[1][:], in_=w1_rows[:, :, W1_CHUNK:H])
+        w1_rows = w1.rearrange("(p j) c -> p j c", j=PACK)
+        w1_raw = [tile([P, PACK, W1_CHUNK], F32, f"w1_raw{c}") for c in range(2)]
+        for c in range(2):
+            nc.sync.dma_start(out=w1_raw[c][:], in_=w1_rows[:, :, W1_CHUNK * c : W1_CHUNK * (c + 1)])
         unit_sb = tile([P, PACK], F32, "unit_sb")
         nc.sync.dma_start(out=unit_sb[:], in_=unit.rearrange("(p t) o -> p (t o)", t=PACK))
         w2_raw = tile([P, PACK, N], F32, "w2_raw")
@@ -74,10 +74,10 @@ def tile_picked_ycatmu_pos_p_kernel(
             )
 
         w1_bf = tile([P, PACK, P, PACK], BF16, "w1_bf")
-        for c in range(2):
+        for c, t0, t1 in ((0, 0, 4), (1, 0, 2), (1, 2, 4)):
             nc.scalar.activation(
-                out=w1_bf[:, :, 64 * c : 64 * c + 64, :].rearrange("p t m j -> p m j t"),
-                in_=w1_raw[c][:].rearrange("p j (m t) -> p m j t", t=PACK),
+                out=w1_bf[:, t0:t1, 64 * c : 64 * c + 64, :].rearrange("p t m j -> p m j t"),
+                in_=w1_raw[c][:].rearrange("p j (m t) -> p m j t", t=PACK)[:, :, :, t0:t1],
                 func=COPY,
             )
         w1_code = tile([P, H], U32, "w1_code")
@@ -106,7 +106,7 @@ def tile_picked_ycatmu_pos_p_kernel(
                 )
 
         w2_bf = tile([P, N, PACK], BF16, "w2_bf")
-        nc.vector.tensor_copy(w2_bf[:], w2_raw[:].rearrange("p j n -> p n j"))
+        nc.scalar.activation(out=w2_bf[:], in_=w2_raw[:].rearrange("p j n -> p n j"), func=COPY)
         w2_code = tile([P, N], U32, "w2_code")
         w2_scale = tile([P, N], U8, "w2_scale")
 
@@ -129,61 +129,73 @@ def tile_picked_ycatmu_pos_p_kernel(
         def face_sums(t):
             nc.vector.tensor_tensor(face[t][:, 0:V], face[t][:, V : 3 * V : 2], face[t][:, V + 1 : 3 * V : 2], ADD)
 
-        def unit_tiles(name, dtype):
-            return {(u, h): tile([P, 2, HALF], dtype, f"{name}{u}{h}") for u in range(2) for h in range(2)}
+        def unit_tiles(name):
+            return {(u, h): tile([P, 2, w], F32, f"{name}{u}{h}") for u in range(2) for h, (r0, w) in enumerate(PIECES)}
 
-        pa, pb, ga, gb = unit_tiles("pa", F32), unit_tiles("pb", F32), unit_tiles("ga", F32), unit_tiles("gb", F32)
-        mid, part, diff, mix = unit_tiles("mid", F32), unit_tiles("part", F32), unit_tiles("diff", F32), unit_tiles("mix", F32)
-        hid_pairs = [tile([P, 2, HALF, 2], BF16, f"hid_pairs{h}") for h in range(2)]
+        mid, diff, mix = unit_tiles("mid"), unit_tiles("diff"), unit_tiles("mix")
+        hid_pairs = [tile([P, 2, w, 2], BF16, f"hid_pairs{h}") for h, (r0, w) in enumerate(PIECES)]
 
         def cols(lst, h):
-            return lst[:, 16 * h : 16 * h + 16]
+            r0, w = PIECES[h]
+            return lst[:, r0 // 16 : (r0 + w) // 16]
 
-        def gather(dst, window, lst, t, h):
-            nc.scalar.activation(out=dst[t // 2, h][:, t % 2, :], in_=window[t][:].indirect(cols(lst, h)), func=COPY)
+        def gather(name, window, lst, t, h, on_vector=False):
+            dst = ring.tile([P, PIECES[h][1]], F32, name=name, align_bytes=64)
+            if on_vector:
+                nc.vector.tensor_copy(dst[:], window[t][:].indirect(cols(lst, h)))
+            else:
+                nc.scalar.activation(out=dst[:], in_=window[t][:].indirect(cols(lst, h)), func=COPY)
+            return dst
 
-        def add_mid(u, h, ts):
-            nc.vector.tensor_tensor(mid[u, h][:, ts, :], pa[u, h][:, ts, :], pb[u, h][:, ts, :], ADD)
+        def edge_step(t, h, fuse_mid, fuse_diff):
+            u, e = t // 2, t % 2
+            pa = gather("pa", y, va_sb, t, h, (t, h) == (0, 0))
+            if fuse_mid:
+                nc.vector.tensor_tensor(mid[u, h][:, e, :], y[t][:].indirect(cols(vb_sb, h)), pa[:], ADD)
+            else:
+                pb = gather("pb", y, vb_sb, t, h)
+                nc.vector.tensor_tensor(mid[u, h][:, e, :], pa[:], pb[:], ADD)
+            ga = gather("ga", face, fa_sb, t, h)
+            part = ring.tile([P, PIECES[h][1]], F32, name="part", align_bytes=64)
+            nc.vector.scalar_tensor_tensor(part[:], mid[u, h][:, e, :], -4.0, ga[:], MULT, ADD)
+            if fuse_diff:
+                nc.vector.tensor_tensor(diff[u, h][:, e, :], face[t][:].indirect(cols(fb_sb, h)), part[:], ADD)
+            else:
+                gb = gather("gb", face, fb_sb, t, h)
+                nc.vector.tensor_tensor(diff[u, h][:, e, :], gb[:], part[:], ADD)
 
-        def sub_mid(u, h, ts):
-            nc.vector.scalar_tensor_tensor(part[u, h][:, ts, :], mid[u, h][:, ts, :], -4.0, ga[u, h][:, ts, :], MULT, ADD)
-
-        def add_face_fused(t, h):
-            u = t // 2
-            nc.vector.tensor_tensor(diff[u, h][:, t % 2, :], face[t][:].indirect(cols(fb_sb, h)), part[u, h][:, t % 2, :], ADD)
-
-        def add_face(u, h):
-            nc.vector.tensor_tensor(diff[u, h][:], gb[u, h][:], part[u, h][:], ADD)
-
-        def sharpen(u, h):
+        def sharpen(u, h, es):
+            r0, w = PIECES[h]
             nc.vector.scalar_tensor_tensor(
-                mix[u, h][:], shp_sb[u][:, :, HALF * h : HALF * (h + 1)], -1.0, diff[u, h][:], ADD, MULT
+                mix[u, h][:, es, :], shp_sb[u][:, es, r0 : r0 + w], -1.0, diff[u, h][:, es, :], ADD, MULT
             )
 
-        def round_pairs(u, h):
+        def round_pairs(u, h, c0, c1):
             nc.vector.scalar_tensor_tensor(
-                hid_pairs[h][:, u, :, :],
-                mid[u, h][:].rearrange("p e r -> p r e"),
+                hid_pairs[h][:, u, c0:c1, :],
+                mid[u, h][:, :, c0:c1].rearrange("p e r -> p r e"),
                 8.0,
-                mix[u, h][:].rearrange("p e r -> p r e"),
+                mix[u, h][:, :, c0:c1].rearrange("p e r -> p r e"),
                 MULT,
                 SUB,
             )
 
-        def decode(h):
-            hid_bf = tile([P, HALF, PACK], BF16, f"hid_bf{h}")
-            nc.vector.tensor_copy(
-                hid_bf[:].rearrange("p r t -> p (r t)").bitcast(I32).rearrange("p (r u) -> p r u", u=2),
-                hid_pairs[h][:].rearrange("p u r e -> p (u r e)").bitcast(I32).rearrange("p (u r) -> p r u", u=2),
+        def decode(h, c0, c1, bank, weave):
+            r0, w = PIECES[h][0] + c0, c1 - c0
+            hid_bf = tile([P, w, PACK], BF16, f"hid_bf{bank}")
+            pair_words = hid_pairs[h][:].rearrange("p u r e -> p (u r e)").bitcast(U32)
+            weave(
+                hid_bf[:].rearrange("p r t -> p (r t)").bitcast(U32).rearrange("p (r u) -> p r u", u=2),
+                pair_words.rearrange("p (u r) -> p r u", u=2)[:, c0:c1, :],
             )
-            hid_code = tile([P, HALF], U32, f"hid_code{h}")
-            hid_scale = tile([P, HALF], U8, f"hid_scale{h}")
+            hid_code = tile([P, w], U32, f"hid_code{bank}")
+            hid_scale = tile([P, w], U8, f"hid_scale{bank}")
             nc.vector.quantize_mx(
                 out=hid_code[:].bitcast(FP8X4), scales=hid_scale[:], in_=hid_bf[:].rearrange("p r t -> p (r t)")
             )
-            acc = psum.tile([P, BANK], F32, name=f"bank{h}")
+            acc = psum.tile([P, BANK], F32, name=f"bank{bank}")
             nc.tensor.matmul_mx(
-                out=acc[:, 0:HALF],
+                out=acc[:, 0:w],
                 lhsT=w2_code[:].bitcast(FP8X4),
                 lhsT_scale=w2_scale[:],
                 rhs=hid_code[:].bitcast(FP8X4),
@@ -191,48 +203,38 @@ def tile_picked_ycatmu_pos_p_kernel(
                 start=True,
                 stop=True,
             )
-            res = tile([P, HALF], F32, f"res{h}")
-            nc.scalar.activation(out=res[:], in_=acc[:, 0:HALF], func=COPY)
-            nc.sync.dma_start(out=out[:, HALF * h : HALF * (h + 1)], in_=res[:])
+            res = tile([P, w], F32, f"res{bank}")
+            nc.scalar.activation(out=res[:], in_=acc[:, 0:w], func=COPY)
+            nc.sync.dma_start(out=out[:, r0 : r0 + w], in_=res[:])
 
-        evacuate(0, 0, False)
-        evacuate(0, 1, True)
+        def weave_on_vector(dst, src):
+            nc.vector.tensor_copy(dst.bitcast(I32), src.bitcast(I32))
+
         nc.vector.quantize_mx(
             out=w2_code[:].bitcast(FP8X4), scales=w2_scale[:], in_=w2_bf[:].rearrange("p n j -> p (n j)")
         )
-        for t in range(PACK):
-            u, one = t // 2, slice(t % 2, t % 2 + 1)
-            face_pairs(t)
-            gather(pa, y, va_sb, t, 0)
-            gather(pb, y, vb_sb, t, 0)
-            if t == 0:
-                evacuate(1, 0, True)
-            face_sums(t)
-            if t == 0:
-                evacuate(1, 1, True)
-            gather(ga, face, fa_sb, t, 0)
-            if 0 < t < PACK - 1:
-                evacuate(t + 1, 0, False)
-                evacuate(t + 1, 1, False)
-            add_mid(u, 0, one)
-            sub_mid(u, 0, one)
-            add_face_fused(t, 0)
-            if t % 2 == 1:
-                sharpen(u, 0)
-                round_pairs(u, 0)
-        decode(0)
-        both = slice(0, 2)
-        for u in range(2):
-            for t in (2 * u, 2 * u + 1):
-                gather(pa, y, va_sb, t, 1)
-                gather(pb, y, vb_sb, t, 1)
-            add_mid(u, 1, both)
-            for t in (2 * u, 2 * u + 1):
-                gather(ga, face, fa_sb, t, 1)
-            sub_mid(u, 1, both)
-            for t in (2 * u, 2 * u + 1):
-                gather(gb, face, fb_sb, t, 1)
-            add_face(u, 1)
-            sharpen(u, 1)
-            round_pairs(u, 1)
-        decode(1)
+        steps = [(t, h) for h in range(len(PIECES)) for t in range(PACK)]
+        for k in range(-2, len(steps)):
+            if k + 2 < PACK:
+                t = k + 2
+                for b in range(2):
+                    evacuate(t, b, (t, b) == (0, 1))
+                face_pairs(t)
+                face_sums(t)
+            if k >= 0:
+                t, h = steps[k]
+                edge_step(t, h, h == 0, h == 0)
+                last = h == len(PIECES) - 1
+                w = PIECES[h][1]
+                if last and t >= 2:
+                    sharpen(t // 2, h, slice(t % 2, t % 2 + 1))
+                elif t % 2 == 1:
+                    sharpen(t // 2, h, slice(0, 2))
+                if t == 1:
+                    round_pairs(0, h, 0, w)
+                if t == 3:
+                    nsub = 2 if last else 1
+                    for c in range(nsub):
+                        round_pairs(1, h, c * w // nsub, (c + 1) * w // nsub)
+                    for c in range(nsub):
+                        decode(h, c * w // nsub, (c + 1) * w // nsub, h + c, nc.scalar.copy if h in () else weave_on_vector)

@@ -17,9 +17,14 @@ COPY = mybir.ActivationFunctionType.Copy
 
 P = 128
 PACK = 4
+LAST = PACK - 1
 BANK = 512
-PIECES = ((0, 256), (256, 256))
+LIST_ROWS = 16
 W1_CHUNK = H // 2
+OUT_PIECE = 128
+FUSED_TILES = 2
+LAST_SPLIT = 256
+PICKED_BUFS = 6
 
 
 def tile_picked_ycatmu_pos_p_kernel(
@@ -28,7 +33,8 @@ def tile_picked_ycatmu_pos_p_kernel(
     nc = tc.nc
     with ExitStack() as ctx:
         keep = ctx.enter_context(tc.tile_pool(name="keep", bufs=1))
-        ring = ctx.enter_context(tc.tile_pool(name="ring", bufs=2))
+        picked_pool = ctx.enter_context(tc.tile_pool(name="picked", bufs=PICKED_BUFS))
+        part_pool = ctx.enter_context(tc.tile_pool(name="part", bufs=3))
         psum = ctx.enter_context(tc.psum_pool(name="psum", bufs=1))
 
         def tile(shape, dtype, name):
@@ -38,6 +44,9 @@ def tile_picked_ycatmu_pos_p_kernel(
             dst = tile([P, src.shape[1]], U16, name)
             nc.sync.dma_start(out=dst[:], in_=src)
             return dst
+
+        def entries(lst, r0, r1):
+            return lst[:, r0 // LIST_ROWS : r1 // LIST_ROWS]
 
         offs_sb = load_list(offs, "offs_sb")
         table_scales = tile([P, T], U8, "table_scales")
@@ -70,13 +79,14 @@ def tile_picked_ycatmu_pos_p_kernel(
         x_code = [tile([P, BANK], U32, f"x_code{b}") for b in range(2)]
         for b in range(2):
             nc.vector.tensor_copy(
-                x_code[b][:], table_words[:].bitcast(U32).indirect(offs_sb[:, 32 * b : 32 * b + 32])
+                x_code[b][:], table_words[:].bitcast(U32).indirect(entries(offs_sb, BANK * b, BANK * (b + 1)))
             )
 
         w1_bf = tile([P, PACK, P, PACK], BF16, "w1_bf")
-        for c, t0, t1 in ((0, 0, 4), (1, 0, 2), (1, 2, 4)):
+        chunk_m = W1_CHUNK // PACK
+        for c, t0, t1 in ((0, 0, PACK), (1, 0, 2), (1, 2, PACK)):
             nc.scalar.activation(
-                out=w1_bf[:, t0:t1, 64 * c : 64 * c + 64, :].rearrange("p t m j -> p m j t"),
+                out=w1_bf[:, t0:t1, chunk_m * c : chunk_m * (c + 1), :].rearrange("p t m j -> p m j t"),
                 in_=w1_raw[c][:].rearrange("p j (m t) -> p m j t", t=PACK)[:, :, :, t0:t1],
                 func=COPY,
             )
@@ -91,111 +101,107 @@ def tile_picked_ycatmu_pos_p_kernel(
         gain = tile([P, PACK], F32, "gain")
         nc.gpsimd.tensor_scalar(gain[:], unit_sb[:], 0.0625, 0.0, MULT, ADD)
 
-        y_psum = {}
-        for t in range(PACK):
-            for b in range(2):
-                y_psum[t, b] = psum.tile([P, BANK], F32, name=f"bank{2 * t + b}")
-                nc.tensor.matmul_mx(
-                    out=y_psum[t, b][:],
-                    lhsT=w1_code[:, P * t : P * (t + 1)].bitcast(FP8X4),
-                    lhsT_scale=w1_scale[:, P * t : P * (t + 1)],
-                    rhs=x_code[b][:].bitcast(FP8X4),
-                    rhs_scale=x_scale[:, BANK * b : BANK * (b + 1)],
-                    start=True,
-                    stop=True,
-                )
+        passes = [(0, c0, BANK // 2) for c0 in range(0, S, BANK // 2)] + [(t, c0, BANK) for t in range(1, PACK) for c0 in range(0, S, BANK)]
+        y_psum = []
+        for i, (t, c0, width) in enumerate(passes):
+            acc = psum.tile([P, BANK], F32, name=f"bank{i % 8}")
+            nc.tensor.matmul_mx(
+                out=acc[:, 0:width],
+                lhsT=w1_code[:, P * t : P * (t + 1)].bitcast(FP8X4),
+                lhsT_scale=w1_scale[:, P * t : P * (t + 1)],
+                rhs=x_code[c0 // BANK][:, c0 % BANK : c0 % BANK + width].bitcast(FP8X4),
+                rhs_scale=x_scale[:, c0 : c0 + width],
+                start=True,
+                stop=True,
+            )
+            y_psum.append(acc)
 
         w2_bf = tile([P, N, PACK], BF16, "w2_bf")
         nc.scalar.activation(out=w2_bf[:], in_=w2_raw[:].rearrange("p j n -> p n j"), func=COPY)
         w2_code = tile([P, N], U32, "w2_code")
         w2_scale = tile([P, N], U8, "w2_scale")
+        nc.vector.quantize_mx(
+            out=w2_code[:].bitcast(FP8X4), scales=w2_scale[:], in_=w2_bf[:].rearrange("p n j -> p (n j)")
+        )
 
         y = [tile([P, S], F32, f"y{t}") for t in range(PACK)]
-        face = [tile([P, V + 2 * V], F32, f"face{t}") for t in range(PACK)]
-
-        def evacuate(t, b, on_vector):
-            dst = y[t][:, BANK * b : BANK * (b + 1)]
-            if on_vector:
-                nc.vector.tensor_scalar(dst, y_psum[t, b][:], gain[:, t : t + 1], None, MULT)
-            else:
-                nc.scalar.activation(out=dst, in_=y_psum[t, b][:], func=COPY, scale=gain[:, t : t + 1])
-
-        def face_pairs(t):
+        sums = [tile([P, V + 2 * V], F32, f"sums{t}") for t in range(PACK)]
+        for t in range(PACK):
+            for i, (t_pass, c0, width) in enumerate(passes):
+                if t_pass != t:
+                    continue
+                if t == 0 and i % 2 == 1:
+                    nc.vector.tensor_scalar(y[t][:, c0 : c0 + width], y_psum[i][:, 0:width], gain[:, t : t + 1], None, MULT)
+                else:
+                    nc.scalar.activation(
+                        out=y[t][:, c0 : c0 + width], in_=y_psum[i][:, 0:width], func=COPY, scale=gain[:, t : t + 1]
+                    )
             quads = y[t][:].rearrange("p (v d) -> p v d", d=D)
-            nc.vector.tensor_tensor(
-                face[t][:, V : 3 * V].rearrange("p (v e) -> p v e", e=2), quads[:, :, 0:2], quads[:, :, 2:4], ADD
-            )
+            halves = sums[t][:, V : 3 * V]
+            nc.vector.tensor_tensor(halves.rearrange("p (v e) -> p v e", e=2), quads[:, :, 0:2], quads[:, :, 2:4], ADD)
+            nc.vector.tensor_tensor(sums[t][:, 0:V], halves[:, 0 : 2 * V : 2], halves[:, 1 : 2 * V : 2], ADD)
 
-        def face_sums(t):
-            nc.vector.tensor_tensor(face[t][:, 0:V], face[t][:, V : 3 * V : 2], face[t][:, V + 1 : 3 * V : 2], ADD)
+        mid, diff, mix = (tile([P, PACK, U], F32, name) for name in ("mid", "diff", "mix"))
+        hid_pairs = tile([P, 2, U, 2], BF16, "hid_pairs")
 
-        def unit_tiles(name):
-            return {(u, h): tile([P, 2, w], F32, f"{name}{u}{h}") for u in range(2) for h, (r0, w) in enumerate(PIECES)}
-
-        mid, diff, mix = unit_tiles("mid"), unit_tiles("diff"), unit_tiles("mix")
-        hid_pairs = [tile([P, 2, w, 2], BF16, f"hid_pairs{h}") for h, (r0, w) in enumerate(PIECES)]
-
-        def cols(lst, h):
-            r0, w = PIECES[h]
-            return lst[:, r0 // 16 : (r0 + w) // 16]
-
-        def gather(name, window, lst, t, h, on_vector=False):
-            dst = ring.tile([P, PIECES[h][1]], F32, name=name, align_bytes=64)
-            if on_vector:
-                nc.vector.tensor_copy(dst[:], window[t][:].indirect(cols(lst, h)))
-            else:
-                nc.scalar.activation(out=dst[:], in_=window[t][:].indirect(cols(lst, h)), func=COPY)
+        def look_up(window, lst, r0, r1):
+            dst = picked_pool.tile([P, r1 - r0], F32, name="picked", align_bytes=64)
+            nc.scalar.activation(out=dst[:], in_=window[:].indirect(entries(lst, r0, r1)), func=COPY)
             return dst
 
-        def edge_step(t, h, fuse_mid, fuse_diff):
-            u, e = t // 2, t % 2
-            pa = gather("pa", y, va_sb, t, h, (t, h) == (0, 0))
-            if fuse_mid:
-                nc.vector.tensor_tensor(mid[u, h][:, e, :], y[t][:].indirect(cols(vb_sb, h)), pa[:], ADD)
+        def points(t):
+            if t == 0:
+                first = tile([P, U], F32, "first")
+                nc.vector.tensor_copy(first[:], y[t][:].indirect(va_sb[:]))
             else:
-                pb = gather("pb", y, vb_sb, t, h)
-                nc.vector.tensor_tensor(mid[u, h][:, e, :], pa[:], pb[:], ADD)
-            ga = gather("ga", face, fa_sb, t, h)
-            part = ring.tile([P, PIECES[h][1]], F32, name="part", align_bytes=64)
-            nc.vector.scalar_tensor_tensor(part[:], mid[u, h][:, e, :], -4.0, ga[:], MULT, ADD)
-            if fuse_diff:
-                nc.vector.tensor_tensor(diff[u, h][:, e, :], face[t][:].indirect(cols(fb_sb, h)), part[:], ADD)
+                first = look_up(y[t], va_sb, 0, U)
+            if t < FUSED_TILES:
+                nc.vector.tensor_tensor(mid[:, t, :], y[t][:].indirect(vb_sb[:]), first[:], ADD)
             else:
-                gb = gather("gb", face, fb_sb, t, h)
-                nc.vector.tensor_tensor(diff[u, h][:, e, :], gb[:], part[:], ADD)
+                nc.vector.tensor_tensor(mid[:, t, :], first[:], look_up(y[t], vb_sb, 0, U)[:], ADD)
 
-        def sharpen(u, h, es):
-            r0, w = PIECES[h]
+        def faces(t, r0, r1, fused):
+            by_fa = look_up(sums[t], fa_sb, r0, r1)
+            part = part_pool.tile([P, r1 - r0], F32, name="part", align_bytes=64)
+            nc.vector.scalar_tensor_tensor(part[:], mid[:, t, r0:r1], -4.0, by_fa[:], MULT, ADD)
+            if fused:
+                nc.vector.tensor_tensor(diff[:, t, r0:r1], sums[t][:].indirect(entries(fb_sb, r0, r1)), part[:], ADD)
+            else:
+                nc.vector.tensor_tensor(diff[:, t, r0:r1], look_up(sums[t], fb_sb, r0, r1)[:], part[:], ADD)
             nc.vector.scalar_tensor_tensor(
-                mix[u, h][:, es, :], shp_sb[u][:, es, r0 : r0 + w], -1.0, diff[u, h][:, es, :], ADD, MULT
+                mix[:, t, r0:r1], shp_sb[t // 2][:, t % 2, r0:r1], -1.0, diff[:, t, r0:r1], ADD, MULT
             )
 
-        def round_pairs(u, h, c0, c1):
+        def round_pair(u, r0, r1):
             nc.vector.scalar_tensor_tensor(
-                hid_pairs[h][:, u, c0:c1, :],
-                mid[u, h][:, :, c0:c1].rearrange("p e r -> p r e"),
+                hid_pairs[:, u, r0:r1, :],
+                mid[:, 2 * u : 2 * u + 2, r0:r1].rearrange("p e r -> p r e"),
                 8.0,
-                mix[u, h][:, :, c0:c1].rearrange("p e r -> p r e"),
+                mix[:, 2 * u : 2 * u + 2, r0:r1].rearrange("p e r -> p r e"),
                 MULT,
                 SUB,
             )
 
-        def decode(h, c0, c1, bank, weave):
-            r0, w = PIECES[h][0] + c0, c1 - c0
-            hid_bf = tile([P, w, PACK], BF16, f"hid_bf{bank}")
-            pair_words = hid_pairs[h][:].rearrange("p u r e -> p (u r e)").bitcast(U32)
-            weave(
-                hid_bf[:].rearrange("p r t -> p (r t)").bitcast(U32).rearrange("p (r u) -> p r u", u=2),
-                pair_words.rearrange("p (u r) -> p r u", u=2)[:, c0:c1, :],
-            )
-            hid_code = tile([P, w], U32, f"hid_code{bank}")
-            hid_scale = tile([P, w], U8, f"hid_scale{bank}")
+        def weave(r0):
+            hid_bf = tile([P, OUT_PIECE, PACK], BF16, f"hid_bf{r0}")
+            dst = hid_bf[:].rearrange("p r t -> p (r t)").bitcast(U32).rearrange("p (r u) -> p r u", u=2)
+            pair_words = hid_pairs[:].rearrange("p u r e -> p (u r e)").bitcast(U32)
+            src = pair_words.rearrange("p (u r) -> p r u", u=2)[:, r0 : r0 + OUT_PIECE, :]
+            if r0 == U - OUT_PIECE:
+                nc.vector.tensor_copy(dst.bitcast(I32), src.bitcast(I32))
+            else:
+                nc.scalar.copy(dst, src)
+            return hid_bf
+
+        def decode(hid_bf, r0):
+            hid_code = tile([P, OUT_PIECE], U32, f"hid_code{r0}")
+            hid_scale = tile([P, OUT_PIECE], U8, f"hid_scale{r0}")
             nc.vector.quantize_mx(
                 out=hid_code[:].bitcast(FP8X4), scales=hid_scale[:], in_=hid_bf[:].rearrange("p r t -> p (r t)")
             )
-            acc = psum.tile([P, BANK], F32, name=f"bank{bank}")
+            acc = psum.tile([P, BANK], F32, name=f"bank{2 + r0 // OUT_PIECE}")
             nc.tensor.matmul_mx(
-                out=acc[:, 0:w],
+                out=acc[:, 0:OUT_PIECE],
                 lhsT=w2_code[:].bitcast(FP8X4),
                 lhsT_scale=w2_scale[:],
                 rhs=hid_code[:].bitcast(FP8X4),
@@ -203,38 +209,21 @@ def tile_picked_ycatmu_pos_p_kernel(
                 start=True,
                 stop=True,
             )
-            res = tile([P, w], F32, f"res{bank}")
-            nc.scalar.activation(out=res[:], in_=acc[:, 0:w], func=COPY)
-            nc.sync.dma_start(out=out[:, r0 : r0 + w], in_=res[:])
+            res = tile([P, OUT_PIECE], F32, f"res{r0}")
+            nc.scalar.activation(out=res[:], in_=acc[:, 0:OUT_PIECE], func=COPY)
+            nc.sync.dma_start(out=out[:, r0 : r0 + OUT_PIECE], in_=res[:])
 
-        def weave_on_vector(dst, src):
-            nc.vector.tensor_copy(dst.bitcast(I32), src.bitcast(I32))
-
-        nc.vector.quantize_mx(
-            out=w2_code[:].bitcast(FP8X4), scales=w2_scale[:], in_=w2_bf[:].rearrange("p n j -> p (n j)")
-        )
-        steps = [(t, h) for h in range(len(PIECES)) for t in range(PACK)]
-        for k in range(-2, len(steps)):
-            if k + 2 < PACK:
-                t = k + 2
-                for b in range(2):
-                    evacuate(t, b, (t, b) == (0, 1))
-                face_pairs(t)
-                face_sums(t)
-            if k >= 0:
-                t, h = steps[k]
-                edge_step(t, h, h == 0, h == 0)
-                last = h == len(PIECES) - 1
-                w = PIECES[h][1]
-                if last and t >= 2:
-                    sharpen(t // 2, h, slice(t % 2, t % 2 + 1))
-                elif t % 2 == 1:
-                    sharpen(t // 2, h, slice(0, 2))
-                if t == 1:
-                    round_pairs(0, h, 0, w)
-                if t == 3:
-                    nsub = 2 if last else 1
-                    for c in range(nsub):
-                        round_pairs(1, h, c * w // nsub, (c + 1) * w // nsub)
-                    for c in range(nsub):
-                        decode(h, c * w // nsub, (c + 1) * w // nsub, h + c, nc.scalar.copy if h in () else weave_on_vector)
+        for t in range(LAST):
+            points(t)
+            faces(t, 0, U, t < FUSED_TILES)
+            if t == 1:
+                round_pair(0, 0, U)
+        points(LAST)
+        for r0, r1 in ((0, LAST_SPLIT), (LAST_SPLIT, U)):
+            faces(LAST, r0, r1, False)
+            pieces = range(r0, r1, OUT_PIECE)
+            for c0 in pieces:
+                round_pair(1, c0, c0 + OUT_PIECE)
+            woven = [weave(c0) for c0 in pieces]
+            for hid_bf, c0 in zip(woven, pieces):
+                decode(hid_bf, c0)

from contextlib import ExitStack

import concourse.mybir as mybir

K, T, S, D, N, H, V, U = 512, 2048, 1024, 4, 128, 512, 256, 512
FLOPS = 2 * K * H * S + 2 * H * N * U

F32 = mybir.dt.float32
BF16 = mybir.dt.bfloat16
I32 = mybir.dt.int32
U32 = mybir.dt.uint32
U16 = mybir.dt.uint16
U8 = mybir.dt.uint8
FP8X4 = mybir.dt.float8_e4m3fn_x4
ADD, SUB, MULT = mybir.AluOpType.add, mybir.AluOpType.subtract, mybir.AluOpType.mult
COPY = mybir.ActivationFunctionType.Copy

P = 128
PACK = 4
LAST = PACK - 1
BANK = 512
LIST_ROWS = 16
W1_CHUNK = H // 2
OUT_PIECE = 128
FUSED_TILES = 2
LAST_SPLIT = 256
PICKED_BUFS = 6


def tile_picked_ycatmu_pos_p_kernel(
    tc, x_words, x_scales, w1, shp, unit, w2, offs, fa, fb, va, vb, out
):
    nc = tc.nc
    with ExitStack() as ctx:
        keep = ctx.enter_context(tc.tile_pool(name="keep", bufs=1))
        picked_pool = ctx.enter_context(tc.tile_pool(name="picked", bufs=PICKED_BUFS))
        part_pool = ctx.enter_context(tc.tile_pool(name="part", bufs=3))
        psum = ctx.enter_context(tc.psum_pool(name="psum", bufs=1))

        def tile(shape, dtype, name):
            return keep.tile(shape, dtype, name=name, align_bytes=64)

        def load_list(src, name):
            dst = tile([P, src.shape[1]], U16, name)
            nc.sync.dma_start(out=dst[:], in_=src)
            return dst

        def entries(lst, r0, r1):
            return lst[:, r0 // LIST_ROWS : r1 // LIST_ROWS]

        offs_sb = load_list(offs, "offs_sb")
        table_scales = tile([P, T], U8, "table_scales")
        for q in range(4):
            nc.sync.dma_start(
                out=table_scales[32 * q : 32 * q + 32, :].bitcast(I32),
                in_=x_scales[0, 4 * q : 4 * q + 4, :].bitcast(I32).partition_broadcast(8),
            )
        table_words = tile([P, T], I32, "table_words")
        nc.sync.dma_start(out=table_words[:], in_=x_words[0].rearrange("p c r -> p (c r)").bitcast(I32))
        w1_rows = w1.rearrange("(p j) c -> p j c", j=PACK)
        w1_raw = [tile([P, PACK, W1_CHUNK], F32, f"w1_raw{c}") for c in range(2)]
        for c in range(2):
            nc.sync.dma_start(out=w1_raw[c][:], in_=w1_rows[:, :, W1_CHUNK * c : W1_CHUNK * (c + 1)])
        unit_sb = tile([P, PACK], F32, "unit_sb")
        nc.sync.dma_start(out=unit_sb[:], in_=unit.rearrange("(p t) o -> p (t o)", t=PACK))
        w2_raw = tile([P, PACK, N], F32, "w2_raw")
        nc.sync.dma_start(out=w2_raw[:], in_=w2.rearrange("(p j) n -> p j n", j=PACK))
        va_sb = load_list(va, "va_sb")
        vb_sb = load_list(vb, "vb_sb")
        fa_sb = load_list(fa, "fa_sb")
        fb_sb = load_list(fb, "fb_sb")
        shp_rows = shp.rearrange("(p t) r -> p t r", t=PACK)
        shp_sb = [tile([P, 2, U], F32, f"shp_sb{u}") for u in range(2)]
        for u in range(2):
            nc.sync.dma_start(out=shp_sb[u][:], in_=shp_rows[:, 2 * u : 2 * u + 2, :])

        x_scale = tile([P, S], U8, "x_scale")
        nc.vector.tensor_copy(x_scale[:], table_scales[:].indirect(offs_sb[:]))
        x_code = [tile([P, BANK], U32, f"x_code{b}") for b in range(2)]
        for b in range(2):
            nc.vector.tensor_copy(
                x_code[b][:], table_words[:].bitcast(U32).indirect(entries(offs_sb, BANK * b, BANK * (b + 1)))
            )

        w1_bf = tile([P, PACK, P, PACK], BF16, "w1_bf")
        chunk_m = W1_CHUNK // PACK
        for c, t0, t1 in ((0, 0, PACK), (1, 0, 2), (1, 2, PACK)):
            nc.scalar.activation(
                out=w1_bf[:, t0:t1, chunk_m * c : chunk_m * (c + 1), :].rearrange("p t m j -> p m j t"),
                in_=w1_raw[c][:].rearrange("p j (m t) -> p m j t", t=PACK)[:, :, :, t0:t1],
                func=COPY,
            )
        w1_code = tile([P, H], U32, "w1_code")
        w1_scale = tile([P, H], U8, "w1_scale")
        for t in range(PACK):
            nc.vector.quantize_mx(
                out=w1_code[:, P * t : P * (t + 1)].bitcast(FP8X4),
                scales=w1_scale[:, P * t : P * (t + 1)],
                in_=w1_bf[:, t, :, :].rearrange("p m j -> p (m j)"),
            )
        gain = tile([P, PACK], F32, "gain")
        nc.gpsimd.tensor_scalar(gain[:], unit_sb[:], 0.0625, 0.0, MULT, ADD)

        passes = [(0, c0, BANK // 2) for c0 in range(0, S, BANK // 2)] + [(t, c0, BANK) for t in range(1, PACK) for c0 in range(0, S, BANK)]
        y_psum = []
        for i, (t, c0, width) in enumerate(passes):
            acc = psum.tile([P, BANK], F32, name=f"bank{i % 8}")
            nc.tensor.matmul_mx(
                out=acc[:, 0:width],
                lhsT=w1_code[:, P * t : P * (t + 1)].bitcast(FP8X4),
                lhsT_scale=w1_scale[:, P * t : P * (t + 1)],
                rhs=x_code[c0 // BANK][:, c0 % BANK : c0 % BANK + width].bitcast(FP8X4),
                rhs_scale=x_scale[:, c0 : c0 + width],
                start=True,
                stop=True,
            )
            y_psum.append(acc)

        w2_bf = tile([P, N, PACK], BF16, "w2_bf")
        nc.scalar.activation(out=w2_bf[:], in_=w2_raw[:].rearrange("p j n -> p n j"), func=COPY)
        w2_code = tile([P, N], U32, "w2_code")
        w2_scale = tile([P, N], U8, "w2_scale")
        nc.vector.quantize_mx(
            out=w2_code[:].bitcast(FP8X4), scales=w2_scale[:], in_=w2_bf[:].rearrange("p n j -> p (n j)")
        )

        y = [tile([P, S], F32, f"y{t}") for t in range(PACK)]
        sums = [tile([P, V + 2 * V], F32, f"sums{t}") for t in range(PACK)]
        for t in range(PACK):
            for i, (t_pass, c0, width) in enumerate(passes):
                if t_pass != t:
                    continue
                if t == 0 and i % 2 == 1:
                    nc.vector.tensor_scalar(y[t][:, c0 : c0 + width], y_psum[i][:, 0:width], gain[:, t : t + 1], None, MULT)
                else:
                    nc.scalar.activation(
                        out=y[t][:, c0 : c0 + width], in_=y_psum[i][:, 0:width], func=COPY, scale=gain[:, t : t + 1]
                    )
            quads = y[t][:].rearrange("p (v d) -> p v d", d=D)
            halves = sums[t][:, V : 3 * V]
            nc.vector.tensor_tensor(halves.rearrange("p (v e) -> p v e", e=2), quads[:, :, 0:2], quads[:, :, 2:4], ADD)
            nc.vector.tensor_tensor(sums[t][:, 0:V], halves[:, 0 : 2 * V : 2], halves[:, 1 : 2 * V : 2], ADD)

        mid, diff, mix = (tile([P, PACK, U], F32, name) for name in ("mid", "diff", "mix"))
        hid_pairs = tile([P, 2, U, 2], BF16, "hid_pairs")

        def look_up(window, lst, r0, r1):
            dst = picked_pool.tile([P, r1 - r0], F32, name="picked", align_bytes=64)
            nc.scalar.activation(out=dst[:], in_=window[:].indirect(entries(lst, r0, r1)), func=COPY)
            return dst

        def points(t):
            if t == 0:
                first = tile([P, U], F32, "first")
                nc.vector.tensor_copy(first[:], y[t][:].indirect(va_sb[:]))
            else:
                first = look_up(y[t], va_sb, 0, U)
            if t < FUSED_TILES:
                nc.vector.tensor_tensor(mid[:, t, :], y[t][:].indirect(vb_sb[:]), first[:], ADD)
            else:
                nc.vector.tensor_tensor(mid[:, t, :], first[:], look_up(y[t], vb_sb, 0, U)[:], ADD)

        def faces(t, r0, r1, fused):
            by_fa = look_up(sums[t], fa_sb, r0, r1)
            part = part_pool.tile([P, r1 - r0], F32, name="part", align_bytes=64)
            nc.vector.scalar_tensor_tensor(part[:], mid[:, t, r0:r1], -4.0, by_fa[:], MULT, ADD)
            if fused:
                nc.vector.tensor_tensor(diff[:, t, r0:r1], sums[t][:].indirect(entries(fb_sb, r0, r1)), part[:], ADD)
            else:
                nc.vector.tensor_tensor(diff[:, t, r0:r1], look_up(sums[t], fb_sb, r0, r1)[:], part[:], ADD)
            nc.vector.scalar_tensor_tensor(
                mix[:, t, r0:r1], shp_sb[t // 2][:, t % 2, r0:r1], -1.0, diff[:, t, r0:r1], ADD, MULT
            )

        def round_pair(u, r0, r1):
            nc.vector.scalar_tensor_tensor(
                hid_pairs[:, u, r0:r1, :],
                mid[:, 2 * u : 2 * u + 2, r0:r1].rearrange("p e r -> p r e"),
                8.0,
                mix[:, 2 * u : 2 * u + 2, r0:r1].rearrange("p e r -> p r e"),
                MULT,
                SUB,
            )

        def weave(r0):
            hid_bf = tile([P, OUT_PIECE, PACK], BF16, f"hid_bf{r0}")
            dst = hid_bf[:].rearrange("p r t -> p (r t)").bitcast(U32).rearrange("p (r u) -> p r u", u=2)
            pair_words = hid_pairs[:].rearrange("p u r e -> p (u r e)").bitcast(U32)
            src = pair_words.rearrange("p (u r) -> p r u", u=2)[:, r0 : r0 + OUT_PIECE, :]
            if r0 == U - OUT_PIECE:
                nc.vector.tensor_copy(dst.bitcast(I32), src.bitcast(I32))
            else:
                nc.scalar.copy(dst, src)
            return hid_bf

        def decode(hid_bf, r0):
            hid_code = tile([P, OUT_PIECE], U32, f"hid_code{r0}")
            hid_scale = tile([P, OUT_PIECE], U8, f"hid_scale{r0}")
            nc.vector.quantize_mx(
                out=hid_code[:].bitcast(FP8X4), scales=hid_scale[:], in_=hid_bf[:].rearrange("p r t -> p (r t)")
            )
            acc = psum.tile([P, BANK], F32, name=f"bank{2 + r0 // OUT_PIECE}")
            nc.tensor.matmul_mx(
                out=acc[:, 0:OUT_PIECE],
                lhsT=w2_code[:].bitcast(FP8X4),
                lhsT_scale=w2_scale[:],
                rhs=hid_code[:].bitcast(FP8X4),
                rhs_scale=hid_scale[:],
                start=True,
                stop=True,
            )
            res = tile([P, OUT_PIECE], F32, f"res{r0}")
            nc.scalar.activation(out=res[:], in_=acc[:, 0:OUT_PIECE], func=COPY)
            nc.sync.dma_start(out=out[:, r0 : r0 + OUT_PIECE], in_=res[:])

        for t in range(LAST):
            points(t)
            faces(t, 0, U, t < FUSED_TILES)
            if t == 1:
                round_pair(0, 0, U)
        points(LAST)
        for r0, r1 in ((0, LAST_SPLIT), (LAST_SPLIT, U)):
            faces(LAST, r0, r1, False)
            pieces = range(r0, r1, OUT_PIECE)
            for c0 in pieces:
                round_pair(1, c0, c0 + OUT_PIECE)
            woven = [weave(c0) for c0 in pieces]
            for hid_bf, c0 in zip(woven, pieces):
                decode(hid_bf, c0)
